import numpy as np
import ml_dtypes


def mxq(x, axis, fmt="e4m3"):
    dtype, down = {"e4m3": (ml_dtypes.float8_e4m3fn, 7), "e5m2": (ml_dtypes.float8_e5m2, 14)}[fmt]
    v = np.moveaxis(np.asarray(x, np.float32).astype(ml_dtypes.bfloat16).astype(np.float64), axis, -1)
    blocks = v.reshape(v.shape[:-1] + (-1, 32))
    amax = np.abs(blocks).max(-1, keepdims=True)
    byte = np.maximum(np.where(amax > 0, np.frexp(amax)[1] - 1 + 127, 0) - down, 1)
    scale = np.exp2(byte - 127.0)
    codes = (blocks / scale).astype(np.float32).astype(dtype).astype(np.float64)
    return np.moveaxis((codes * scale).reshape(v.shape), -1, axis)


WIDE = False


def mx_kscale(k):
    if not WIDE:
        return np.ones(k)
    levels = np.array([10, -10, 5, -5, 0])
    if k % 512:
        return np.exp2(np.random.permutation(np.resize(levels, k // 32))).repeat(32)
    a = np.empty((k // 512, 16))
    for p in range(k // 512):
        a[p, :8] = np.random.permutation(np.resize(levels, 8))
        for g in range(8):
            far = levels[np.abs(levels - a[p, g]) >= 10]
            a[p, g + 8] = far[np.random.randint(len(far))]
    return np.exp2(a.ravel()).repeat(32)


def f64(x):
    return np.asarray(x).astype(np.float64)


def striped8(idx):
    return np.asarray(idx).reshape(8, -1, 16).transpose(0, 2, 1).reshape(128, -1).astype(np.uint16)


def unstriped8(offs):
    return offs.reshape(8, 16, -1).transpose(0, 2, 1).reshape(8, -1).astype(np.int64)


def pick8(x, idx, run):
    r = np.arange(len(x))
    return x[r[:, None], idx[r % (8 * run) // run]]


E2M1 = np.array([0.0, 0.5, 1.0, 1.5, 2.0, 3.0, 4.0, 6.0, -0.0, -0.5, -1.0, -1.5, -2.0, -3.0, -4.0, -6.0])


def pack_weight(w, fmt):
    k, n = w.shape
    w = f64(np.asarray(w, np.float32).astype(ml_dtypes.bfloat16)).reshape(k // 32, 32, n)
    amax = np.abs(w).max(1)
    if fmt == "e4m3":
        byte = np.frexp(amax)[1] - 1 + 127 - 7
    else:
        mant, ex = np.frexp(amax / 6.0)
        byte = np.where(mant > 0.5, ex, ex - 1) + 127
    byte = np.clip(np.where(amax > 0, byte, 1), 1, 254)
    scaled = (w * np.exp2(127.0 - byte)[:, None, :]).reshape(k, n).astype(np.float32)
    by_word = np.ascontiguousarray(scaled.reshape(k // 512, 128, 4, n).transpose(0, 1, 3, 2))
    if fmt == "e4m3":
        words = by_word.astype(ml_dtypes.float8_e4m3fn).view(np.uint8)
    else:
        c = by_word.astype(ml_dtypes.float4_e2m1fn).view(np.uint8) & 0xF
        words = (c[..., 0::2] | (c[..., 1::2] << 4)).reshape(k // 512, 128, 2 * n)
    return np.ascontiguousarray(words), np.ascontiguousarray(byte.astype(np.uint8).reshape(k // 512, 16, n))


def unpack_weight(words, scales, fmt):
    g, _, n = scales.shape
    words = np.ascontiguousarray(words).reshape(g, 128, n, -1)
    if fmt == "e4m3":
        vals = words.view(ml_dtypes.float8_e4m3fn).astype(np.float64)
    else:
        nib = np.empty((g, 128, n, 4), np.uint8)
        nib[..., 0::2] = words & 0xF
        nib[..., 1::2] = words >> 4
        vals = E2M1[nib]
    vals = vals * np.repeat(np.exp2(scales.astype(np.float64) - 127.0), 8, axis=1)[..., None]
    return vals.transpose(0, 1, 3, 2).reshape(g * 512, n)


D, T, Z, I, Q, E = 512, 1024, 1024, 512, 512, 256


def setup_inputs():
    n = np.random.standard_normal
    idx = np.stack([np.random.permutation(T)[:I] for _ in range(8)])
    idx2 = np.stack([np.random.permutation(T)[:I] for _ in range(8)])
    idx3 = np.stack([np.random.permutation(T)[:I] for _ in range(8)])
    idx4 = np.stack([np.random.permutation(Z)[:I] for _ in range(8)])
    idx5 = np.stack([np.random.permutation(Z)[:I] for _ in range(8)])
    fd = mx_kscale(D)
    fq = mx_kscale(Q)
    cachep = pack_weight(n((D, T)) / fd[:, None], "e4m3")
    mixp = pack_weight(n((Q, E)) * 1.0 / np.sqrt(Q) / fq[:, None], "e2m1")
    return {
        "query": (n((D, Q)) * 1.0 / np.sqrt(D) * fd[:, None]).astype(np.float32),
        "cache_words": cachep[0],
        "cache_scales": cachep[1],
        "rowf": (np.random.uniform(0.5, 2.0, (Q, 1)) * fq[:, None]).astype(np.float32),
        "mix_words": mixp[0],
        "mix_scales": mixp[1],
        "offs": striped8(idx),
        "offs2": striped8(idx2),
        "offs3": striped8(idx3),
        "offs4": striped8(idx4),
        "offs5": striped8(idx5),
    }


def reference(query, cache_words, cache_scales, rowf, mix_words, mix_scales, offs, offs2, offs3, offs4, offs5):
    idx = unstriped8(offs)
    idx2 = unstriped8(offs2)
    idx3 = unstriped8(offs3)
    idx4 = unstriped8(offs4)
    idx5 = unstriped8(offs5)
    cacheu = unpack_weight(cache_words, cache_scales, "e4m3")
    mixu = unpack_weight(mix_words, mix_scales, "e2m1")
    queryq = mxq(f64(query), 0, "e4m3")
    a = queryq.T @ cacheu
    f1 = np.zeros((Q, T))
    f1[np.arange(Q)[:, None], idx2[np.arange(Q) % 512 // 64]] = pick8(a, idx, 64)
    c1 = np.maximum(a, f1)
    g = pick8(c1, idx3, 64) - pick8(a, idx, 64)
    gw = g * f64(rowf)
    gwq = mxq(gw, 0, "e4m3")
    o1 = mixu.T @ gwq
    pa = np.zeros((E, Z))
    pa[np.arange(E)[:, None], idx4[np.arange(E) % 128 // 16]] = o1
    y = pick8(pa, idx5, 16) - o1
    return y

@@ -1,0 +1,258 @@
+from contextlib import ExitStack
+
+import concourse.mybir as mybir
+
+D, T, Z, I, Q, E = 512, 1024, 1024, 512, 512, 256
+FLOPS = 2 * D * Q * T + 2 * Q * E * I
+
+F32 = mybir.dt.float32
+BF16 = mybir.dt.bfloat16
+I32 = mybir.dt.int32
+U32 = mybir.dt.uint32
+U16 = mybir.dt.uint16
+U8 = mybir.dt.uint8
+FP8X4 = mybir.dt.float8_e4m3fn_x4
+FP4X4 = mybir.dt.float4_e2m1fn_x4
+COPY = mybir.ActivationFunctionType.Copy
+MULT = mybir.AluOpType.mult
+SUB = mybir.AluOpType.subtract
+MAX = mybir.AluOpType.max
+
+P = 128
+PACK = 4
+BANK = 512
+HALF = I // 2
+LIST_COLS = I // 16
+Q_HALF = Q // 2
+M_HALF = Q_HALF // PACK
+M_VECTOR = 40
+
+
+def tile_attend_overlaid_one_posted_kernel(
+    tc, query, cache_words, cache_scales, rowf, mix_words, mix_scales, offs, offs2, offs3, offs4, offs5, out
+):
+    nc = tc.nc
+    with ExitStack() as ctx:
+        keep = ctx.enter_context(tc.tile_pool(name="keep", bufs=1))
+        psum = ctx.enter_context(tc.psum_pool(name="psum", bufs=8))
+
+        def slots(h):
+            return slice(h * HALF, (h + 1) * HALF)
+
+        def entries(lst, h):
+            return lst[:, h * (LIST_COLS // 2) : (h + 1) * (LIST_COLS // 2)]
+
+        cs_rows = keep.tile([4, 4, T // 4], I32, name="cs_rows")
+        nc.sync.dma_start(out=cs_rows[:], in_=cache_scales[0].bitcast(I32).rearrange("(g r) c -> r g c", r=4))
+        q_rows = query.rearrange("(p j) q -> p j q", j=PACK)
+        q_raw = []
+        for h in range(2):
+            raw = keep.tile([P, PACK, Q_HALF], F32, name="q_raw%d" % h)
+            nc.sync.dma_start(out=raw[:], in_=q_rows[:, :, h * Q_HALF : (h + 1) * Q_HALF])
+            q_raw.append(raw)
+        cw_rows = cache_words[0].rearrange("p n t -> p (n t)").bitcast(I32)
+        c_words = []
+        for h in range(2):
+            words = keep.tile([P, BANK], U32, name="c_words%d" % h, align_bytes=64)
+            nc.sync.dma_start(out=words[:].bitcast(I32), in_=cw_rows[:, h * BANK : (h + 1) * BANK])
+            c_words.append(words)
+        lists = []
+        for n, src in enumerate((offs, offs2, offs3)):
+            lst = keep.tile([P, LIST_COLS], U16, name="list%d" % n)
+            nc.sync.dma_start(lst[:], src)
+            lists.append(lst)
+        rf = keep.tile([P, PACK], F32, name="rf")
+        nc.sync.dma_start(out=rf[:], in_=rowf.rearrange("(p t) o -> p (t o)", t=PACK))
+        m_words = keep.tile([P, 2 * E], U8, name="m_words", align_bytes=64)
+        nc.sync.dma_start(out=m_words[:].bitcast(I32), in_=mix_words[0].bitcast(I32))
+        for n, src in enumerate((offs4, offs5)):
+            lst = keep.tile([P, LIST_COLS], U16, name="list%d" % (n + 3))
+            nc.sync.dma_start(lst[:], src)
+            lists.append(lst)
+        pick, post, pick3, post4, pick5 = lists
+
+        c_scales = keep.tile([P, T], U8, name="c_scales", align_bytes=64)
+        m_scales = keep.tile([P, E], U8, name="m_scales", align_bytes=64)
+        nc.vector.memset(c_scales[:].bitcast(I32), 0)
+        nc.vector.memset(m_scales[:].bitcast(I32), 0)
+        for g in range(4):
+            nc.sync.dma_start(
+                out=m_scales[32 * g : 32 * g + 4, :].bitcast(I32), in_=mix_scales[0, 4 * g : 4 * g + 4, :].bitcast(I32)
+            )
+        f1 = [keep.tile([P, T], F32, name="f1_%d" % n) for n in range(2)]
+        pa = [keep.tile([P, Z], F32, name="pa_%d" % n) for n in range(2)]
+        for window in f1:
+            nc.vector.memset(window[:], 0.0)
+        for g in range(4):
+            nc.vector.tensor_copy(out=c_scales[32 * g : 32 * g + 4, :].bitcast(I32), in_=cs_rows[:, g, :])
+        for window in pa:
+            nc.vector.memset(window[:], 0.0)
+
+        q_bf = keep.tile([P, PACK, P, PACK], BF16, name="q_bf", align_bytes=64)
+
+        def deal(h, m0, m1):
+            dst = q_bf[:, :, h * M_HALF + m0 : h * M_HALF + m1, :].rearrange("p t m j -> p m t j")
+            src = q_raw[h][:, :, PACK * m0 : PACK * m1].rearrange("p j (m t) -> p m t j", t=PACK)
+            return dst, src
+
+        dst, src = deal(0, 0, M_HALF)
+        nc.scalar.activation(dst, src, COPY)
+        dst, src = deal(1, 0, M_VECTOR)
+        nc.vector.tensor_copy(out=dst, in_=src)
+        dst, src = deal(1, M_VECTOR, M_HALF)
+        nc.scalar.activation(dst, src, COPY)
+
+        q_words = keep.tile([P, Q], U32, name="q_words", align_bytes=64)
+        q_scales = keep.tile([P, Q], U8, name="q_scales", align_bytes=64)
+
+        def quantise_query(t0, t1):
+            nc.vector.quantize_mx(
+                out=q_words[:, t0 * P : t1 * P].bitcast(FP8X4),
+                scales=q_scales[:, t0 * P : t1 * P],
+                in_=q_bf[:, t0:t1, :, :].rearrange("p t m j -> p (t m j)"),
+            )
+
+        banks = {}
+
+        def score(t):
+            for h in range(2):
+                bank = psum.tile([P, BANK], F32, name="bank", tag="bank")
+                nc.tensor.matmul_mx(
+                    out=bank[:],
+                    lhsT=q_words[:, t * P : (t + 1) * P].bitcast(FP8X4),
+                    lhsT_scale=q_scales[:, t * P : (t + 1) * P],
+                    rhs=c_words[h][:].bitcast(FP8X4),
+                    rhs_scale=c_scales[:, h * BANK : (h + 1) * BANK],
+                    start=True,
+                    stop=True,
+                )
+                banks[(t, h)] = bank
+
+        a = [keep.tile([P, T], F32, name="a_%d" % t) for t in range(PACK)]
+        c1 = [keep.tile([P, T], F32, name="c1_%d" % t) for t in range(PACK)]
+        ga = [keep.tile([P, I], F32, name="ga_%d" % t) for t in range(PACK)]
+        g = [[keep.tile([P, HALF], F32, name="g_%d_%d" % (t, h)) for h in range(2)] for t in range(PACK)]
+        gw = [keep.tile([P, HALF, PACK], BF16, name="gw_%d" % h, align_bytes=64) for h in range(2)]
+
+        def empty_v(t, h):
+            nc.vector.tensor_copy(out=a[t][:, h * BANK : (h + 1) * BANK], in_=banks[(t, h)][:])
+
+        def empty_s(t, h):
+            nc.scalar.copy(out=a[t][:, h * BANK : (h + 1) * BANK], in_=banks[(t, h)][:])
+
+        def gather_a(t):
+            nc.vector.tensor_copy(ga[t][:], a[t][:].indirect(pick[:]))
+
+        def scatter_f1(t):
+            nc.scalar.activation(f1[t % 2][:].indirect(post[:]), ga[t][:], COPY)
+
+        def larger(t):
+            nc.vector.tensor_tensor(c1[t][:], a[t][:], f1[t % 2][:], MAX)
+
+        def diff_v(t, h):
+            nc.vector.tensor_tensor(g[t][h][:], c1[t][:].indirect(entries(pick3, h)), ga[t][:, slots(h)], SUB)
+
+        def weigh(t, h):
+            nc.vector.tensor_scalar(gw[h][:, :, t], g[t][h][:], rf[:, t : t + 1], None, op0=MULT)
+
+        quantise_query(0, 1)
+        score(0)
+        quantise_query(1, 2)
+        score(1)
+        empty_v(0, 0)
+        empty_s(0, 1)
+        quantise_query(2, 4)
+        score(2)
+        score(3)
+        empty_s(1, 0)
+        empty_s(1, 1)
+        for h in range(2):
+            nc.vector.tensor_copy(ga[0][:, slots(h)], a[0][:].indirect(entries(pick, h)))
+            nc.scalar.activation(f1[0][:].indirect(entries(post, h)), ga[0][:, slots(h)], COPY)
+        empty_v(2, 0)
+        empty_v(2, 1)
+        gather_a(1)
+        scatter_f1(1)
+        gather_a(2)
+        larger(0)
+        scatter_f1(2)
+        empty_v(3, 0)
+        empty_v(3, 1)
+        diff_v(0, 0)
+        gather_a(3)
+        larger(1)
+        scatter_f1(3)
+        weigh(0, 0)
+        diff_v(1, 0)
+        larger(2)
+        weigh(1, 0)
+        diff_v(2, 0)
+        diff_v(0, 1)
+        larger(3)
+        weigh(2, 0)
+        diff_v(3, 0)
+
+        picked = {}
+        for t in range(1, PACK):
+            x = keep.tile([P, HALF], F32, name="picked_%d" % t)
+            nc.scalar.activation(x[:], c1[t][:].indirect(entries(pick3, 1)), COPY)
+            picked[t] = x
+
+        def diff_plain(t):
+            nc.vector.tensor_tensor(g[t][1][:], picked[t][:], ga[t][:, slots(1)], SUB)
+
+        gw_words = [keep.tile([P, HALF], U32, name="gw_words%d" % h, align_bytes=64) for h in range(2)]
+        gw_scales = [keep.tile([P, HALF], U8, name="gw_scales%d" % h, align_bytes=64) for h in range(2)]
+        o1 = [keep.tile([P, I], F32, name="o1_%d" % j) for j in range(2)]
+
+        def quantise_gw(h):
+            nc.vector.quantize_mx(
+                out=gw_words[h][:].bitcast(FP8X4), scales=gw_scales[h][:], in_=gw[h][:].rearrange("p i t -> p (i t)")
+            )
+
+        def mix(j, h):
+            bank = psum.tile([P, BANK], F32, name="bank", tag="bank")
+            nc.tensor.matmul_mx(
+                out=bank[:, 0:HALF],
+                lhsT=m_words[:, 2 * P * j : 2 * P * (j + 1)].bitcast(FP4X4),
+                lhsT_scale=m_scales[:, P * j : P * (j + 1)],
+                rhs=gw_words[h][:].bitcast(FP8X4),
+                rhs_scale=gw_scales[h][:],
+                start=True,
+                stop=True,
+            )
+            return bank
+
+        def scatter_pa(j, h):
+            nc.scalar.activation(pa[j][:].indirect(entries(post4, h)), o1[j][:, slots(h)], COPY)
+
+        diff_plain(1)
+        weigh(3, 0)
+        diff_plain(2)
+        quantise_gw(0)
+        first = [mix(j, 0) for j in range(2)]
+        for j in range(2):
+            nc.scalar.copy(out=o1[j][:, slots(0)], in_=first[j][:, 0:HALF])
+        for j in range(2):
+            scatter_pa(j, 0)
+        weigh(0, 1)
+        diff_plain(3)
+        weigh(1, 1)
+        weigh(2, 1)
+        weigh(3, 1)
+        quantise_gw(1)
+        second = [mix(j, 1) for j in range(2)]
+        for j in range(2):
+            nc.vector.tensor_copy(out=o1[j][:, slots(1)], in_=second[j][:, 0:HALF])
+        for j in range(2):
+            scatter_pa(j, 1)
+
+        y0 = keep.tile([P, I], F32, name="y0")
+        nc.vector.tensor_tensor(y0[:], pa[0][:].indirect(pick5[:]), o1[0][:], SUB)
+        nc.sync.dma_start(out=out[0:P, :], in_=y0[:])
+        y1 = keep.tile([P, I], F32, name="y1")
+        last = keep.tile([P, HALF], F32, name="last")
+        nc.scalar.activation(last[:], pa[1][:].indirect(entries(pick5, 1)), COPY)
+        nc.vector.tensor_tensor(y1[:, slots(0)], pa[1][:].indirect(entries(pick5, 0)), o1[1][:, slots(0)], SUB)
+        nc.vector.tensor_tensor(y1[:, slots(1)], last[:], o1[1][:, slots(1)], SUB)
+        nc.sync.dma_start(out=out[P : 2 * P, :], in_=y1[:])

@@ -23,9 +23,8 @@ PACK = 4
 BANK = 512
 HALF = I // 2
 LIST_COLS = I // 16
-Q_HALF = Q // 2
-M_HALF = Q_HALF // PACK
-M_VECTOR = 40
+Q_LOADS = ((0, 56), (56, 104), (104, 128))
+PIECE = 128
 
 
 def tile_attend_overlaid_one_posted_kernel(
@@ -34,7 +33,7 @@ def tile_attend_overlaid_one_posted_kernel(
     nc = tc.nc
     with ExitStack() as ctx:
         keep = ctx.enter_context(tc.tile_pool(name="keep", bufs=1))
-        psum = ctx.enter_context(tc.psum_pool(name="psum", bufs=8))
+        psum = ctx.enter_context(tc.psum_pool(name="psum", bufs=1))
 
         def slots(h):
             return slice(h * HALF, (h + 1) * HALF)
@@ -42,14 +41,22 @@ def tile_attend_overlaid_one_posted_kernel(
         def entries(lst, h):
             return lst[:, h * (LIST_COLS // 2) : (h + 1) * (LIST_COLS // 2)]
 
-        cs_rows = keep.tile([4, 4, T // 4], I32, name="cs_rows")
-        nc.sync.dma_start(out=cs_rows[:], in_=cache_scales[0].bitcast(I32).rearrange("(g r) c -> r g c", r=4))
+        c_scales = keep.tile([P, T], U8, name="c_scales", align_bytes=64)
+        m_scales = keep.tile([P, E], U8, name="m_scales", align_bytes=64)
+
+        def load_scales(queue, plane, rows):
+            for quad in range(4):
+                queue.dma_start(
+                    out=plane[32 * quad : 32 * quad + 4, :].bitcast(I32), in_=rows[4 * quad : 4 * quad + 4, :].bitcast(I32)
+                )
+
         q_rows = query.rearrange("(p j) q -> p j q", j=PACK)
         q_raw = []
-        for h in range(2):
-            raw = keep.tile([P, PACK, Q_HALF], F32, name="q_raw%d" % h)
-            nc.sync.dma_start(out=raw[:], in_=q_rows[:, :, h * Q_HALF : (h + 1) * Q_HALF])
+        for n, (m0, m1) in enumerate(Q_LOADS):
+            raw = keep.tile([P, PACK, PACK * (m1 - m0)], F32, name="q_raw%d" % n)
+            nc.sync.dma_start(out=raw[:], in_=q_rows[:, :, PACK * m0 : PACK * m1])
             q_raw.append(raw)
+        load_scales(nc.scalar, c_scales, cache_scales[0])
         cw_rows = cache_words[0].rearrange("p n t -> p (n t)").bitcast(I32)
         c_words = []
         for h in range(2):
@@ -57,50 +64,34 @@ def tile_attend_overlaid_one_posted_kernel(
             nc.sync.dma_start(out=words[:].bitcast(I32), in_=cw_rows[:, h * BANK : (h + 1) * BANK])
             c_words.append(words)
         lists = []
-        for n, src in enumerate((offs, offs2, offs3)):
+        for n, src in enumerate((offs, offs2, offs3, offs4, offs5)):
             lst = keep.tile([P, LIST_COLS], U16, name="list%d" % n)
             nc.sync.dma_start(lst[:], src)
             lists.append(lst)
+        pick, post, pick3, post4, pick5 = lists
         rf = keep.tile([P, PACK], F32, name="rf")
         nc.sync.dma_start(out=rf[:], in_=rowf.rearrange("(p t) o -> p (t o)", t=PACK))
         m_words = keep.tile([P, 2 * E], U8, name="m_words", align_bytes=64)
         nc.sync.dma_start(out=m_words[:].bitcast(I32), in_=mix_words[0].bitcast(I32))
-        for n, src in enumerate((offs4, offs5)):
-            lst = keep.tile([P, LIST_COLS], U16, name="list%d" % (n + 3))
-            nc.sync.dma_start(lst[:], src)
-            lists.append(lst)
-        pick, post, pick3, post4, pick5 = lists
+        load_scales(nc.sync, m_scales, mix_scales[0])
 
-        c_scales = keep.tile([P, T], U8, name="c_scales", align_bytes=64)
-        m_scales = keep.tile([P, E], U8, name="m_scales", align_bytes=64)
-        nc.vector.memset(c_scales[:].bitcast(I32), 0)
-        nc.vector.memset(m_scales[:].bitcast(I32), 0)
-        for g in range(4):
-            nc.sync.dma_start(
-                out=m_scales[32 * g : 32 * g + 4, :].bitcast(I32), in_=mix_scales[0, 4 * g : 4 * g + 4, :].bitcast(I32)
-            )
         f1 = [keep.tile([P, T], F32, name="f1_%d" % n) for n in range(2)]
         pa = [keep.tile([P, Z], F32, name="pa_%d" % n) for n in range(2)]
-        for window in f1:
-            nc.vector.memset(window[:], 0.0)
-        for g in range(4):
-            nc.vector.tensor_copy(out=c_scales[32 * g : 32 * g + 4, :].bitcast(I32), in_=cs_rows[:, g, :])
-        for window in pa:
+        for window in f1 + pa:
             nc.vector.memset(window[:], 0.0)
 
         q_bf = keep.tile([P, PACK, P, PACK], BF16, name="q_bf", align_bytes=64)
 
-        def deal(h, m0, m1):
-            dst = q_bf[:, :, h * M_HALF + m0 : h * M_HALF + m1, :].rearrange("p t m j -> p m t j")
-            src = q_raw[h][:, :, PACK * m0 : PACK * m1].rearrange("p j (m t) -> p m t j", t=PACK)
-            return dst, src
+        def deal(n, m0, m1, t0, t1):
+            base = Q_LOADS[n][0]
+            dst = q_bf[:, t0:t1, m0:m1, :].rearrange("p t m j -> p m t j")
+            src = q_raw[n][:, :, PACK * (m0 - base) : PACK * (m1 - base)].rearrange("p j (m t) -> p m t j", t=PACK)
+            return dst, src[:, :, t0:t1, :]
 
-        dst, src = deal(0, 0, M_HALF)
-        nc.scalar.activation(dst, src, COPY)
-        dst, src = deal(1, 0, M_VECTOR)
-        nc.vector.tensor_copy(out=dst, in_=src)
-        dst, src = deal(1, M_VECTOR, M_HALF)
-        nc.scalar.activation(dst, src, COPY)
+        for n, (m0, m1) in enumerate(Q_LOADS):
+            mid = (m0 + m1) // 2
+            nc.vector.tensor_copy(*deal(n, m0, mid, 0, PACK))
+            nc.scalar.activation(*deal(n, mid, m1, 0, PACK), COPY)
 
         q_words = keep.tile([P, Q], U32, name="q_words", align_bytes=64)
         q_scales = keep.tile([P, Q], U8, name="q_scales", align_bytes=64)
@@ -116,7 +107,8 @@ def tile_attend_overlaid_one_posted_kernel(
 
         def score(t):
             for h in range(2):
-                bank = psum.tile([P, BANK], F32, name="bank", tag="bank")
+                tag = "first_bank" if (t, h) == (0, 0) else "score_bank%d" % h
+                bank = psum.tile([P, BANK], F32, name=tag, tag=tag)
                 nc.tensor.matmul_mx(
                     out=bank[:],
                     lhsT=q_words[:, t * P : (t + 1) * P].bitcast(FP8X4),
@@ -128,11 +120,10 @@ def tile_attend_overlaid_one_posted_kernel(
                 )
                 banks[(t, h)] = bank
 
-        a = [keep.tile([P, T], F32, name="a_%d" % t) for t in range(PACK)]
+        a = [keep.tile([P, T], F32, name="a_%d" % t, tag="a_%d" % t) for t in range(PACK)]
         c1 = [keep.tile([P, T], F32, name="c1_%d" % t) for t in range(PACK)]
         ga = [keep.tile([P, I], F32, name="ga_%d" % t) for t in range(PACK)]
-        g = [[keep.tile([P, HALF], F32, name="g_%d_%d" % (t, h)) for h in range(2)] for t in range(PACK)]
-        gw = [keep.tile([P, HALF, PACK], BF16, name="gw_%d" % h, align_bytes=64) for h in range(2)]
+        g = [keep.tile([P, PACK, HALF], F32, name="g_%d" % h) for h in range(2)]
 
         def empty_v(t, h):
             nc.vector.tensor_copy(out=a[t][:, h * BANK : (h + 1) * BANK], in_=banks[(t, h)][:])
@@ -150,109 +141,115 @@ def tile_attend_overlaid_one_posted_kernel(
             nc.vector.tensor_tensor(c1[t][:], a[t][:], f1[t % 2][:], MAX)
 
         def diff_v(t, h):
-            nc.vector.tensor_tensor(g[t][h][:], c1[t][:].indirect(entries(pick3, h)), ga[t][:, slots(h)], SUB)
+            nc.vector.tensor_tensor(g[h][:, t, :], c1[t][:].indirect(entries(pick3, h)), ga[t][:, slots(h)], SUB)
 
-        def weigh(t, h):
-            nc.vector.tensor_scalar(gw[h][:, :, t], g[t][h][:], rf[:, t : t + 1], None, op0=MULT)
+        gw = {
+            lo: keep.tile([P, hi - lo, PACK], BF16, name="gw_%d" % lo, tag="gw", align_bytes=64)
+            for lo, hi in ((0, PIECE), (PIECE, HALF), (HALF, I))
+        }
+
+        def weigh(lo, hi, t0=0, t1=PACK):
+            h = lo // HALF
+            nc.vector.tensor_tensor(
+                gw[lo][:, :, t0:t1].rearrange("p (c i) t -> p c t i", i=4),
+                g[h][:, t0:t1, lo - h * HALF : hi - h * HALF].rearrange("p t (c i) -> p c t i", i=4),
+                rf[:, t0:t1].unsqueeze(1).unsqueeze(3).broadcast_to([P, (hi - lo) // 4, t1 - t0, 4]),
+                MULT,
+            )
 
         quantise_query(0, 1)
+        quantise_query(1, 4)
         score(0)
-        quantise_query(1, 2)
+        empty_s(0, 0)
+        empty_v(0, 1)
         score(1)
-        empty_v(0, 0)
-        empty_s(0, 1)
-        quantise_query(2, 4)
-        score(2)
-        score(3)
         empty_s(1, 0)
-        empty_s(1, 1)
         for h in range(2):
             nc.vector.tensor_copy(ga[0][:, slots(h)], a[0][:].indirect(entries(pick, h)))
             nc.scalar.activation(f1[0][:].indirect(entries(post, h)), ga[0][:, slots(h)], COPY)
+        empty_v(1, 1)
+        score(2)
         empty_v(2, 0)
-        empty_v(2, 1)
         gather_a(1)
         scatter_f1(1)
-        gather_a(2)
+        empty_v(2, 1)
+        score(3)
         larger(0)
+        gather_a(2)
         scatter_f1(2)
         empty_v(3, 0)
         empty_v(3, 1)
-        diff_v(0, 0)
-        gather_a(3)
         larger(1)
+        gather_a(3)
         scatter_f1(3)
-        weigh(0, 0)
-        diff_v(1, 0)
+        diff_v(0, 0)
         larger(2)
-        weigh(1, 0)
+        diff_v(1, 0)
         diff_v(2, 0)
-        diff_v(0, 1)
+        weigh(0, PIECE, 0, 2)
         larger(3)
-        weigh(2, 0)
         diff_v(3, 0)
 
-        picked = {}
-        for t in range(1, PACK):
-            x = keep.tile([P, HALF], F32, name="picked_%d" % t)
-            nc.scalar.activation(x[:], c1[t][:].indirect(entries(pick3, 1)), COPY)
-            picked[t] = x
+        picked = keep.tile([P, PACK, HALF], F32, name="picked", tag="a_2")
+        for t in range(PACK):
+            nc.scalar.activation(picked[:, t, :], c1[t][:].indirect(entries(pick3, 1)), COPY)
 
         def diff_plain(t):
-            nc.vector.tensor_tensor(g[t][1][:], picked[t][:], ga[t][:, slots(1)], SUB)
+            nc.vector.tensor_tensor(g[1][:, t, :], picked[:, t, :], ga[t][:, slots(1)], SUB)
 
-        gw_words = [keep.tile([P, HALF], U32, name="gw_words%d" % h, align_bytes=64) for h in range(2)]
-        gw_scales = [keep.tile([P, HALF], U8, name="gw_scales%d" % h, align_bytes=64) for h in range(2)]
+        gw_words = keep.tile([P, I], U32, name="gw_words", align_bytes=64)
+        gw_scales = keep.tile([P, I], U8, name="gw_scales", align_bytes=64)
         o1 = [keep.tile([P, I], F32, name="o1_%d" % j) for j in range(2)]
 
-        def quantise_gw(h):
+        def quantise_gw(lo, hi):
             nc.vector.quantize_mx(
-                out=gw_words[h][:].bitcast(FP8X4), scales=gw_scales[h][:], in_=gw[h][:].rearrange("p i t -> p (i t)")
+                out=gw_words[:, lo:hi].bitcast(FP8X4), scales=gw_scales[:, lo:hi], in_=gw[lo][:].rearrange("p i t -> p (i t)")
             )
 
-        def mix(j, h):
-            bank = psum.tile([P, BANK], F32, name="bank", tag="bank")
+        def mix(j, lo, hi):
+            bank = psum.tile([P, BANK], F32, name="mix_bank", tag="mix_bank", bufs=5)
             nc.tensor.matmul_mx(
-                out=bank[:, 0:HALF],
+                out=bank[:, 0 : hi - lo],
                 lhsT=m_words[:, 2 * P * j : 2 * P * (j + 1)].bitcast(FP4X4),
                 lhsT_scale=m_scales[:, P * j : P * (j + 1)],
-                rhs=gw_words[h][:].bitcast(FP8X4),
-                rhs_scale=gw_scales[h][:],
+                rhs=gw_words[:, lo:hi].bitcast(FP8X4),
+                rhs_scale=gw_scales[:, lo:hi],
                 start=True,
                 stop=True,
             )
-            return bank
+            return o1[j][:, lo:hi], bank[:, 0 : hi - lo]
 
-        def scatter_pa(j, h):
-            nc.scalar.activation(pa[j][:].indirect(entries(post4, h)), o1[j][:, slots(h)], COPY)
+        def scatter_pa(j, lo, hi):
+            nc.scalar.activation(pa[j][:].indirect(post4[:, lo // 16 : hi // 16]), o1[j][:, lo:hi], COPY)
 
+        diff_plain(0)
+        weigh(0, PIECE, 2, PACK)
         diff_plain(1)
-        weigh(3, 0)
+        quantise_gw(0, PIECE)
+        for j in range(2):
+            nc.scalar.copy(*mix(j, 0, PIECE))
+        for j in range(2):
+            scatter_pa(j, 0, PIECE)
+        weigh(PIECE, HALF)
         diff_plain(2)
-        quantise_gw(0)
-        first = [mix(j, 0) for j in range(2)]
-        for j in range(2):
-            nc.scalar.copy(out=o1[j][:, slots(0)], in_=first[j][:, 0:HALF])
-        for j in range(2):
-            scatter_pa(j, 0)
-        weigh(0, 1)
+        quantise_gw(PIECE, HALF)
         diff_plain(3)
-        weigh(1, 1)
-        weigh(2, 1)
-        weigh(3, 1)
-        quantise_gw(1)
-        second = [mix(j, 1) for j in range(2)]
         for j in range(2):
-            nc.vector.tensor_copy(out=o1[j][:, slots(1)], in_=second[j][:, 0:HALF])
+            nc.vector.tensor_copy(*mix(j, PIECE, HALF))
+            scatter_pa(j, PIECE, HALF)
+        weigh(HALF, I)
+        quantise_gw(HALF, I)
         for j in range(2):
-            scatter_pa(j, 1)
+            nc.vector.tensor_copy(*mix(j, HALF, I))
+            scatter_pa(j, HALF, I)
 
         y0 = keep.tile([P, I], F32, name="y0")
         nc.vector.tensor_tensor(y0[:], pa[0][:].indirect(pick5[:]), o1[0][:], SUB)
         nc.sync.dma_start(out=out[0:P, :], in_=y0[:])
-        y1 = keep.tile([P, I], F32, name="y1")
+        y1 = [keep.tile([P, HALF], F32, name="y1_%d" % h) for h in range(2)]
         last = keep.tile([P, HALF], F32, name="last")
         nc.scalar.activation(last[:], pa[1][:].indirect(entries(pick5, 1)), COPY)
-        nc.vector.tensor_tensor(y1[:, slots(0)], pa[1][:].indirect(entries(pick5, 0)), o1[1][:, slots(0)], SUB)
-        nc.vector.tensor_tensor(y1[:, slots(1)], last[:], o1[1][:, slots(1)], SUB)
-        nc.sync.dma_start(out=out[P : 2 * P, :], in_=y1[:])
+        nc.vector.tensor_tensor(y1[0][:], pa[1][:].indirect(entries(pick5, 0)), o1[1][:, slots(0)], SUB)
+        nc.sync.dma_start(out=out[P : 2 * P, slots(0)], in_=y1[0][:])
+        nc.vector.tensor_tensor(y1[1][:], last[:], o1[1][:, slots(1)], SUB)
+        nc.sync.dma_start(out=out[P : 2 * P, slots(1)], in_=y1[1][:])

@@ -23,7 +23,7 @@ PACK = 4
 BANK = 512
 HALF = I // 2
 LIST_COLS = I // 16
-Q_LOADS = ((0, 56), (56, 104), (104, 128))
+Q_LOADS = ((0, 80), (80, 128))
 PIECE = 128
 
 
@@ -56,13 +56,13 @@ def tile_attend_overlaid_one_posted_kernel(
             raw = keep.tile([P, PACK, PACK * (m1 - m0)], F32, name="q_raw%d" % n)
             nc.sync.dma_start(out=raw[:], in_=q_rows[:, :, PACK * m0 : PACK * m1])
             q_raw.append(raw)
-        load_scales(nc.scalar, c_scales, cache_scales[0])
         cw_rows = cache_words[0].rearrange("p n t -> p (n t)").bitcast(I32)
         c_words = []
         for h in range(2):
             words = keep.tile([P, BANK], U32, name="c_words%d" % h, align_bytes=64)
             nc.sync.dma_start(out=words[:].bitcast(I32), in_=cw_rows[:, h * BANK : (h + 1) * BANK])
             c_words.append(words)
+        load_scales(nc.sync, c_scales, cache_scales[0])
         lists = []
         for n, src in enumerate((offs, offs2, offs3, offs4, offs5)):
             lst = keep.tile([P, LIST_COLS], U16, name="list%d" % n)
@@ -151,9 +151,9 @@ def tile_attend_overlaid_one_posted_kernel(
         def weigh(lo, hi, t0=0, t1=PACK):
             h = lo // HALF
             nc.vector.tensor_tensor(
-                gw[lo][:, :, t0:t1].rearrange("p (c i) t -> p c t i", i=4),
-                g[h][:, t0:t1, lo - h * HALF : hi - h * HALF].rearrange("p t (c i) -> p c t i", i=4),
-                rf[:, t0:t1].unsqueeze(1).unsqueeze(3).broadcast_to([P, (hi - lo) // 4, t1 - t0, 4]),
+                gw[lo][:, :, t0:t1].rearrange("p (c i) t -> p c t i", i=2),
+                g[h][:, t0:t1, lo - h * HALF : hi - h * HALF].rearrange("p t (c i) -> p c t i", i=2),
+                rf[:, t0:t1].unsqueeze(1).unsqueeze(3).broadcast_to([P, (hi - lo) // 2, t1 - t0, 2]),
                 MULT,
             )
 
@@ -186,7 +186,6 @@ def tile_attend_overlaid_one_posted_kernel(
         larger(2)
         diff_v(1, 0)
         diff_v(2, 0)
-        weigh(0, PIECE, 0, 2)
         larger(3)
         diff_v(3, 0)
 
@@ -223,7 +222,7 @@ def tile_attend_overlaid_one_posted_kernel(
             nc.scalar.activation(pa[j][:].indirect(post4[:, lo // 16 : hi // 16]), o1[j][:, lo:hi], COPY)
 
         diff_plain(0)
-        weigh(0, PIECE, 2, PACK)
+        weigh(0, PIECE)
         diff_plain(1)
         quantise_gw(0, PIECE)
         for j in range(2):

@@ -89,7 +89,7 @@ def tile_attend_overlaid_one_posted_kernel(
             return dst, src[:, :, t0:t1, :]
 
         for n, (m0, m1) in enumerate(Q_LOADS):
-            mid = (m0 + m1) // 2
+            mid = m0 + (m1 - m0) // 6 * 4
             nc.vector.tensor_copy(*deal(n, m0, mid, 0, PACK))
             nc.scalar.activation(*deal(n, mid, m1, 0, PACK), COPY)
 
@@ -103,33 +103,27 @@ def tile_attend_overlaid_one_posted_kernel(
                 in_=q_bf[:, t0:t1, :, :].rearrange("p t m j -> p (t m j)"),
             )
 
-        banks = {}
-
-        def score(t):
-            for h in range(2):
-                tag = "first_bank" if (t, h) == (0, 0) else "score_bank%d" % h
-                bank = psum.tile([P, BANK], F32, name=tag, tag=tag)
-                nc.tensor.matmul_mx(
-                    out=bank[:],
-                    lhsT=q_words[:, t * P : (t + 1) * P].bitcast(FP8X4),
-                    lhsT_scale=q_scales[:, t * P : (t + 1) * P],
-                    rhs=c_words[h][:].bitcast(FP8X4),
-                    rhs_scale=c_scales[:, h * BANK : (h + 1) * BANK],
-                    start=True,
-                    stop=True,
-                )
-                banks[(t, h)] = bank
+        def score(t, lo, hi):
+            h = lo // BANK
+            bank = psum.tile([P, BANK], F32, name="score_bank", tag="score_bank", bufs=3)
+            nc.tensor.matmul_mx(
+                out=bank[:, 0 : hi - lo],
+                lhsT=q_words[:, t * P : (t + 1) * P].bitcast(FP8X4),
+                lhsT_scale=q_scales[:, t * P : (t + 1) * P],
+                rhs=c_words[h][:, lo - h * BANK : hi - h * BANK].bitcast(FP8X4),
+                rhs_scale=c_scales[:, lo:hi],
+                start=True,
+                stop=True,
+            )
+            return a[t][:, lo:hi], bank[:, 0 : hi - lo]
 
         a = [keep.tile([P, T], F32, name="a_%d" % t, tag="a_%d" % t) for t in range(PACK)]
         c1 = [keep.tile([P, T], F32, name="c1_%d" % t) for t in range(PACK)]
         ga = [keep.tile([P, I], F32, name="ga_%d" % t) for t in range(PACK)]
         g = [keep.tile([P, PACK, HALF], F32, name="g_%d" % h) for h in range(2)]
 
-        def empty_v(t, h):
-            nc.vector.tensor_copy(out=a[t][:, h * BANK : (h + 1) * BANK], in_=banks[(t, h)][:])
-
-        def empty_s(t, h):
-            nc.scalar.copy(out=a[t][:, h * BANK : (h + 1) * BANK], in_=banks[(t, h)][:])
+        def score_half(t, h):
+            nc.vector.tensor_copy(*score(t, h * BANK, (h + 1) * BANK))
 
         def gather_a(t):
             nc.vector.tensor_copy(ga[t][:], a[t][:].indirect(pick[:]))
@@ -144,14 +138,15 @@ def tile_attend_overlaid_one_posted_kernel(
             nc.vector.tensor_tensor(g[h][:, t, :], c1[t][:].indirect(entries(pick3, h)), ga[t][:, slots(h)], SUB)
 
         gw = {
-            lo: keep.tile([P, hi - lo, PACK], BF16, name="gw_%d" % lo, tag="gw", align_bytes=64)
+            lo: keep.tile([P, hi - lo, PACK], BF16, name="gw_%d" % lo, tag="gw_%d" % (lo // HALF), align_bytes=64)
             for lo, hi in ((0, PIECE), (PIECE, HALF), (HALF, I))
         }
 
         def weigh(lo, hi, t0=0, t1=PACK):
             h = lo // HALF
+            base = min(lo, HALF)
             nc.vector.tensor_tensor(
-                gw[lo][:, :, t0:t1].rearrange("p (c i) t -> p c t i", i=2),
+                gw[base][:, lo - base : hi - base, t0:t1].rearrange("p (c i) t -> p c t i", i=2),
                 g[h][:, t0:t1, lo - h * HALF : hi - h * HALF].rearrange("p t (c i) -> p c t i", i=2),
                 rf[:, t0:t1].unsqueeze(1).unsqueeze(3).broadcast_to([P, (hi - lo) // 2, t1 - t0, 2]),
                 MULT,
@@ -159,26 +154,23 @@ def tile_attend_overlaid_one_posted_kernel(
 
         quantise_query(0, 1)
         quantise_query(1, 4)
-        score(0)
-        empty_s(0, 0)
-        empty_v(0, 1)
-        score(1)
-        empty_s(1, 0)
-        for h in range(2):
-            nc.vector.tensor_copy(ga[0][:, slots(h)], a[0][:].indirect(entries(pick, h)))
-            nc.scalar.activation(f1[0][:].indirect(entries(post, h)), ga[0][:, slots(h)], COPY)
-        empty_v(1, 1)
-        score(2)
-        empty_v(2, 0)
+        nc.scalar.copy(*score(0, 0, BANK))
+        nc.vector.tensor_copy(*score(0, BANK, BANK + HALF))
+        nc.vector.tensor_copy(*score(0, BANK + HALF, T))
+        nc.vector.tensor_copy(ga[0][:, slots(0)], a[0][:].indirect(entries(pick, 0)))
+        nc.scalar.activation(ga[0][:, slots(1)], a[0][:].indirect(entries(pick, 1)), COPY)
+        scatter_f1(0)
+        score_half(1, 0)
+        score_half(1, 1)
+        score_half(2, 0)
         gather_a(1)
         scatter_f1(1)
-        empty_v(2, 1)
-        score(3)
+        score_half(2, 1)
         larger(0)
         gather_a(2)
         scatter_f1(2)
-        empty_v(3, 0)
-        empty_v(3, 1)
+        score_half(3, 0)
+        score_half(3, 1)
         larger(1)
         gather_a(3)
         scatter_f1(3)
@@ -186,6 +178,7 @@ def tile_attend_overlaid_one_posted_kernel(
         larger(2)
         diff_v(1, 0)
         diff_v(2, 0)
+        weigh(0, PIECE, 0, 2)
         larger(3)
         diff_v(3, 0)
 
@@ -222,7 +215,7 @@ def tile_attend_overlaid_one_posted_kernel(
             nc.scalar.activation(pa[j][:].indirect(post4[:, lo // 16 : hi // 16]), o1[j][:, lo:hi], COPY)
 
         diff_plain(0)
-        weigh(0, PIECE)
+        weigh(0, PIECE, 2, PACK)
         diff_plain(1)
         quantise_gw(0, PIECE)
         for j in range(2):
@@ -233,10 +226,11 @@ def tile_attend_overlaid_one_posted_kernel(
         diff_plain(2)
         quantise_gw(PIECE, HALF)
         diff_plain(3)
+        weigh(HALF, HALF + PIECE)
         for j in range(2):
             nc.vector.tensor_copy(*mix(j, PIECE, HALF))
             scatter_pa(j, PIECE, HALF)
-        weigh(HALF, I)
+        weigh(HALF + PIECE, I)
         quantise_gw(HALF, I)
         for j in range(2):
             nc.vector.tensor_copy(*mix(j, HALF, I))

from contextlib import ExitStack

import concourse.mybir as mybir

D, T, Z, I, Q, E = 512, 1024, 1024, 512, 512, 256
FLOPS = 2 * D * Q * T + 2 * Q * E * I

F32 = mybir.dt.float32
BF16 = mybir.dt.bfloat16
I32 = mybir.dt.int32
U32 = mybir.dt.uint32
U16 = mybir.dt.uint16
U8 = mybir.dt.uint8
FP8X4 = mybir.dt.float8_e4m3fn_x4
FP4X4 = mybir.dt.float4_e2m1fn_x4
COPY = mybir.ActivationFunctionType.Copy
MULT = mybir.AluOpType.mult
SUB = mybir.AluOpType.subtract
MAX = mybir.AluOpType.max

P = 128
PACK = 4
BANK = 512
HALF = I // 2
LIST_COLS = I // 16
Q_LOADS = ((0, 80), (80, 128))
PIECE = 128


def tile_attend_overlaid_one_posted_kernel(
    tc, query, cache_words, cache_scales, rowf, mix_words, mix_scales, offs, offs2, offs3, offs4, offs5, out
):
    nc = tc.nc
    with ExitStack() as ctx:
        keep = ctx.enter_context(tc.tile_pool(name="keep", bufs=1))
        psum = ctx.enter_context(tc.psum_pool(name="psum", bufs=1))

        def slots(h):
            return slice(h * HALF, (h + 1) * HALF)

        def entries(lst, h):
            return lst[:, h * (LIST_COLS // 2) : (h + 1) * (LIST_COLS // 2)]

        c_scales = keep.tile([P, T], U8, name="c_scales", align_bytes=64)
        m_scales = keep.tile([P, E], U8, name="m_scales", align_bytes=64)

        def load_scales(queue, plane, rows):
            for quad in range(4):
                queue.dma_start(
                    out=plane[32 * quad : 32 * quad + 4, :].bitcast(I32), in_=rows[4 * quad : 4 * quad + 4, :].bitcast(I32)
                )

        q_rows = query.rearrange("(p j) q -> p j q", j=PACK)
        q_raw = []
        for n, (m0, m1) in enumerate(Q_LOADS):
            raw = keep.tile([P, PACK, PACK * (m1 - m0)], F32, name="q_raw%d" % n)
            nc.sync.dma_start(out=raw[:], in_=q_rows[:, :, PACK * m0 : PACK * m1])
            q_raw.append(raw)
        cw_rows = cache_words[0].rearrange("p n t -> p (n t)").bitcast(I32)
        c_words = []
        for h in range(2):
            words = keep.tile([P, BANK], U32, name="c_words%d" % h, align_bytes=64)
            nc.sync.dma_start(out=words[:].bitcast(I32), in_=cw_rows[:, h * BANK : (h + 1) * BANK])
            c_words.append(words)
        load_scales(nc.sync, c_scales, cache_scales[0])
        lists = []
        for n, src in enumerate((offs, offs2, offs3, offs4, offs5)):
            lst = keep.tile([P, LIST_COLS], U16, name="list%d" % n)
            nc.sync.dma_start(lst[:], src)
            lists.append(lst)
        pick, post, pick3, post4, pick5 = lists
        rf = keep.tile([P, PACK], F32, name="rf")
        nc.sync.dma_start(out=rf[:], in_=rowf.rearrange("(p t) o -> p (t o)", t=PACK))
        m_words = keep.tile([P, 2 * E], U8, name="m_words", align_bytes=64)
        nc.sync.dma_start(out=m_words[:].bitcast(I32), in_=mix_words[0].bitcast(I32))
        load_scales(nc.sync, m_scales, mix_scales[0])

        f1 = [keep.tile([P, T], F32, name="f1_%d" % n) for n in range(2)]
        pa = [keep.tile([P, Z], F32, name="pa_%d" % n) for n in range(2)]
        for window in f1 + pa:
            nc.vector.memset(window[:], 0.0)

        q_bf = keep.tile([P, PACK, P, PACK], BF16, name="q_bf", align_bytes=64)

        def deal(n, m0, m1, t0, t1):
            base = Q_LOADS[n][0]
            dst = q_bf[:, t0:t1, m0:m1, :].rearrange("p t m j -> p m t j")
            src = q_raw[n][:, :, PACK * (m0 - base) : PACK * (m1 - base)].rearrange("p j (m t) -> p m t j", t=PACK)
            return dst, src[:, :, t0:t1, :]

        for n, (m0, m1) in enumerate(Q_LOADS):
            mid = m0 + (m1 - m0) // 6 * 4
            nc.vector.tensor_copy(*deal(n, m0, mid, 0, PACK))
            nc.scalar.activation(*deal(n, mid, m1, 0, PACK), COPY)

        q_words = keep.tile([P, Q], U32, name="q_words", align_bytes=64)
        q_scales = keep.tile([P, Q], U8, name="q_scales", align_bytes=64)

        def quantise_query(t0, t1):
            nc.vector.quantize_mx(
                out=q_words[:, t0 * P : t1 * P].bitcast(FP8X4),
                scales=q_scales[:, t0 * P : t1 * P],
                in_=q_bf[:, t0:t1, :, :].rearrange("p t m j -> p (t m j)"),
            )

        def score(t, lo, hi):
            h = lo // BANK
            bank = psum.tile([P, BANK], F32, name="score_bank", tag="score_bank", bufs=3)
            nc.tensor.matmul_mx(
                out=bank[:, 0 : hi - lo],
                lhsT=q_words[:, t * P : (t + 1) * P].bitcast(FP8X4),
                lhsT_scale=q_scales[:, t * P : (t + 1) * P],
                rhs=c_words[h][:, lo - h * BANK : hi - h * BANK].bitcast(FP8X4),
                rhs_scale=c_scales[:, lo:hi],
                start=True,
                stop=True,
            )
            return a[t][:, lo:hi], bank[:, 0 : hi - lo]

        a = [keep.tile([P, T], F32, name="a_%d" % t, tag="a_%d" % t) for t in range(PACK)]
        c1 = [keep.tile([P, T], F32, name="c1_%d" % t) for t in range(PACK)]
        ga = [keep.tile([P, I], F32, name="ga_%d" % t) for t in range(PACK)]
        g = [keep.tile([P, PACK, HALF], F32, name="g_%d" % h) for h in range(2)]

        def score_half(t, h):
            nc.vector.tensor_copy(*score(t, h * BANK, (h + 1) * BANK))

        def gather_a(t):
            nc.vector.tensor_copy(ga[t][:], a[t][:].indirect(pick[:]))

        def scatter_f1(t):
            nc.scalar.activation(f1[t % 2][:].indirect(post[:]), ga[t][:], COPY)

        def larger(t):
            nc.vector.tensor_tensor(c1[t][:], a[t][:], f1[t % 2][:], MAX)

        def diff_v(t, h):
            nc.vector.tensor_tensor(g[h][:, t, :], c1[t][:].indirect(entries(pick3, h)), ga[t][:, slots(h)], SUB)

        gw = {
            lo: keep.tile([P, hi - lo, PACK], BF16, name="gw_%d" % lo, tag="gw_%d" % (lo // HALF), align_bytes=64)
            for lo, hi in ((0, PIECE), (PIECE, HALF), (HALF, I))
        }

        def weigh(lo, hi, t0=0, t1=PACK):
            h = lo // HALF
            base = min(lo, HALF)
            nc.vector.tensor_tensor(
                gw[base][:, lo - base : hi - base, t0:t1].rearrange("p (c i) t -> p c t i", i=2),
                g[h][:, t0:t1, lo - h * HALF : hi - h * HALF].rearrange("p t (c i) -> p c t i", i=2),
                rf[:, t0:t1].unsqueeze(1).unsqueeze(3).broadcast_to([P, (hi - lo) // 2, t1 - t0, 2]),
                MULT,
            )

        quantise_query(0, 1)
        quantise_query(1, 4)
        nc.scalar.copy(*score(0, 0, BANK))
        nc.vector.tensor_copy(*score(0, BANK, BANK + HALF))
        nc.vector.tensor_copy(*score(0, BANK + HALF, T))
        nc.vector.tensor_copy(ga[0][:, slots(0)], a[0][:].indirect(entries(pick, 0)))
        nc.scalar.activation(ga[0][:, slots(1)], a[0][:].indirect(entries(pick, 1)), COPY)
        scatter_f1(0)
        score_half(1, 0)
        score_half(1, 1)
        score_half(2, 0)
        gather_a(1)
        scatter_f1(1)
        score_half(2, 1)
        larger(0)
        gather_a(2)
        scatter_f1(2)
        score_half(3, 0)
        score_half(3, 1)
        larger(1)
        gather_a(3)
        scatter_f1(3)
        diff_v(0, 0)
        larger(2)
        diff_v(1, 0)
        diff_v(2, 0)
        weigh(0, PIECE, 0, 2)
        larger(3)
        diff_v(3, 0)

        picked = keep.tile([P, PACK, HALF], F32, name="picked", tag="a_2")
        for t in range(PACK):
            nc.scalar.activation(picked[:, t, :], c1[t][:].indirect(entries(pick3, 1)), COPY)

        def diff_plain(t):
            nc.vector.tensor_tensor(g[1][:, t, :], picked[:, t, :], ga[t][:, slots(1)], SUB)

        gw_words = keep.tile([P, I], U32, name="gw_words", align_bytes=64)
        gw_scales = keep.tile([P, I], U8, name="gw_scales", align_bytes=64)
        o1 = [keep.tile([P, I], F32, name="o1_%d" % j) for j in range(2)]

        def quantise_gw(lo, hi):
            nc.vector.quantize_mx(
                out=gw_words[:, lo:hi].bitcast(FP8X4), scales=gw_scales[:, lo:hi], in_=gw[lo][:].rearrange("p i t -> p (i t)")
            )

        def mix(j, lo, hi):
            bank = psum.tile([P, BANK], F32, name="mix_bank", tag="mix_bank", bufs=5)
            nc.tensor.matmul_mx(
                out=bank[:, 0 : hi - lo],
                lhsT=m_words[:, 2 * P * j : 2 * P * (j + 1)].bitcast(FP4X4),
                lhsT_scale=m_scales[:, P * j : P * (j + 1)],
                rhs=gw_words[:, lo:hi].bitcast(FP8X4),
                rhs_scale=gw_scales[:, lo:hi],
                start=True,
                stop=True,
            )
            return o1[j][:, lo:hi], bank[:, 0 : hi - lo]

        def scatter_pa(j, lo, hi):
            nc.scalar.activation(pa[j][:].indirect(post4[:, lo // 16 : hi // 16]), o1[j][:, lo:hi], COPY)

        diff_plain(0)
        weigh(0, PIECE, 2, PACK)
        diff_plain(1)
        quantise_gw(0, PIECE)
        for j in range(2):
            nc.scalar.copy(*mix(j, 0, PIECE))
        for j in range(2):
            scatter_pa(j, 0, PIECE)
        weigh(PIECE, HALF)
        diff_plain(2)
        quantise_gw(PIECE, HALF)
        diff_plain(3)
        weigh(HALF, HALF + PIECE)
        for j in range(2):
            nc.vector.tensor_copy(*mix(j, PIECE, HALF))
            scatter_pa(j, PIECE, HALF)
        weigh(HALF + PIECE, I)
        quantise_gw(HALF, I)
        for j in range(2):
            nc.vector.tensor_copy(*mix(j, HALF, I))
            scatter_pa(j, HALF, I)

        y0 = keep.tile([P, I], F32, name="y0")
        nc.vector.tensor_tensor(y0[:], pa[0][:].indirect(pick5[:]), o1[0][:], SUB)
        nc.sync.dma_start(out=out[0:P, :], in_=y0[:])
        y1 = [keep.tile([P, HALF], F32, name="y1_%d" % h) for h in range(2)]
        last = keep.tile([P, HALF], F32, name="last")
        nc.scalar.activation(last[:], pa[1][:].indirect(entries(pick5, 1)), COPY)
        nc.vector.tensor_tensor(y1[0][:], pa[1][:].indirect(entries(pick5, 0)), o1[1][:, slots(0)], SUB)
        nc.sync.dma_start(out=out[P : 2 * P, slots(0)], in_=y1[0][:])
        nc.vector.tensor_tensor(y1[1][:], last[:], o1[1][:, slots(1)], SUB)
        nc.sync.dma_start(out=out[P : 2 * P, slots(1)], in_=y1[1][:])
